import numpy as np
import ml_dtypes


def mxq(x, axis, fmt="e4m3"):
    dtype, down = {"e4m3": (ml_dtypes.float8_e4m3fn, 7), "e5m2": (ml_dtypes.float8_e5m2, 14)}[fmt]
    v = np.moveaxis(np.asarray(x, np.float32).astype(ml_dtypes.bfloat16).astype(np.float64), axis, -1)
    blocks = v.reshape(v.shape[:-1] + (-1, 32))
    amax = np.abs(blocks).max(-1, keepdims=True)
    byte = np.maximum(np.where(amax > 0, np.frexp(amax)[1] - 1 + 127, 0) - down, 1)
    scale = np.exp2(byte - 127.0)
    codes = (blocks / scale).astype(np.float32).astype(dtype).astype(np.float64)
    return np.moveaxis((codes * scale).reshape(v.shape), -1, axis)


WIDE = False


def mx_kscale(k):
    if not WIDE:
        return np.ones(k)
    levels = np.array([30, -30])
    if k % 512:
        return np.exp2(np.random.permutation(np.resize(levels, k // 32))).repeat(32)
    a = np.empty((k // 512, 16))
    for p in range(k // 512):
        a[p, :8] = np.random.permutation(np.resize(levels, 8))
        for g in range(8):
            far = levels[np.abs(levels - a[p, g]) >= 10]
            a[p, g + 8] = far[np.random.randint(len(far))]
    return np.exp2(a.ravel()).repeat(32)


def f64(x):
    return np.asarray(x).astype(np.float64)


def striped(idx):
    return np.tile(np.asarray(idx).reshape(-1, 16).T, (8, 1)).astype(np.uint16)


def unstriped(offs):
    return offs[:16].T.reshape(-1).astype(np.int64)


E2M1 = np.array([0.0, 0.5, 1.0, 1.5, 2.0, 3.0, 4.0, 6.0, -0.0, -0.5, -1.0, -1.5, -2.0, -3.0, -4.0, -6.0])


def pack_weight(w, fmt):
    k, n = w.shape
    w = f64(np.asarray(w, np.float32).astype(ml_dtypes.bfloat16)).reshape(k // 32, 32, n)
    amax = np.abs(w).max(1)
    if fmt in ("e4m3", "e5m2"):
        byte = np.frexp(amax)[1] - 1 + 127 - (7 if fmt == "e4m3" else 14)
    else:
        mant, ex = np.frexp(amax / 6.0)
        byte = np.where(mant > 0.5, ex, ex - 1) + 127
    byte = np.clip(np.where(amax > 0, byte, 1), 1, 254)
    scaled = (w * np.exp2(127.0 - byte)[:, None, :]).reshape(k, n).astype(np.float32)
    by_word = np.ascontiguousarray(scaled.reshape(k // 512, 128, 4, n).transpose(0, 1, 3, 2))
    if fmt in ("e4m3", "e5m2"):
        words = by_word.astype(ml_dtypes.float8_e4m3fn if fmt == "e4m3" else ml_dtypes.float8_e5m2).view(np.uint8)
    else:
        c = by_word.astype(ml_dtypes.float4_e2m1fn).view(np.uint8) & 0xF
        words = (c[..., 0::2] | (c[..., 1::2] << 4)).reshape(k // 512, 128, 2 * n)
    return np.ascontiguousarray(words), np.ascontiguousarray(byte.astype(np.uint8).reshape(k // 512, 16, n))


def unpack_weight(words, scales, fmt):
    g, _, n = scales.shape
    words = np.ascontiguousarray(words).reshape(g, 128, n, -1)
    if fmt in ("e4m3", "e5m2"):
        vals = words.view(ml_dtypes.float8_e4m3fn if fmt == "e4m3" else ml_dtypes.float8_e5m2).astype(np.float64)
    else:
        nib = np.empty((g, 128, n, 4), np.uint8)
        nib[..., 0::2] = words & 0xF
        nib[..., 1::2] = words >> 4
        vals = E2M1[nib]
    vals = vals * np.repeat(np.exp2(scales.astype(np.float64) - 127.0), 8, axis=1)[..., None]
    return vals.transpose(0, 1, 3, 2).reshape(g * 512, n)


K, T, I, J, N, Z, S, V, O = 512, 1024, 512, 256, 256, 1024, 1024, 1024, 128


def setup_inputs():
    n = np.random.standard_normal
    idx = np.random.permutation(T)[:I]
    idx2 = np.random.permutation(Z)[:J]
    idx3 = np.random.permutation(V)[:J]
    idx4 = np.random.permutation(J)[:O]
    idx5 = np.random.permutation(J)[:O]
    idx6 = np.random.permutation(S)[:N]
    fk = mx_kscale(K)
    fi = mx_kscale(I)
    ti = np.ones(T)
    ti[idx] = fi
    xkp = pack_weight(n((K, T)) * 0.3 * fk[:, None] * ti, "e4m3")
    xqp = pack_weight(n((K, Z)) * 0.3 / fk[:, None], "e2m1")
    xrp = pack_weight(n((K, V)) * 0.3 / fk[:, None], "e5m2")
    vsp = pack_weight(n((I, S)) / fi[:, None], "e2m1")
    return {
        "xk_words": xkp[0],
        "xk_scales": xkp[1],
        "xq_words": xqp[0],
        "xq_scales": xqp[1],
        "xr_words": xrp[0],
        "xr_scales": xrp[1],
        "vs_words": vsp[0],
        "vs_scales": vsp[1],
        "offs": striped(idx),
        "offs2": striped(idx2),
        "offs3": striped(idx3),
        "offs4": striped(idx4),
        "offs5": striped(idx5),
        "offs6": striped(idx6),
    }


def reference(xk_words, xk_scales, xq_words, xq_scales, xr_words, xr_scales, vs_words, vs_scales, offs, offs2, offs3, offs4, offs5, offs6):
    idx = unstriped(offs)
    idx2 = unstriped(offs2)
    idx3 = unstriped(offs3)
    idx4 = unstriped(offs4)
    idx5 = unstriped(offs5)
    idx6 = unstriped(offs6)
    xku = unpack_weight(xk_words, xk_scales, "e4m3")
    xqu = unpack_weight(xq_words, xq_scales, "e2m1")
    xru = unpack_weight(xr_words, xr_scales, "e5m2")
    vsu = unpack_weight(vs_words, vs_scales, "e2m1")
    xkidxg = xku[:, idx]
    xqidx2g = xqu[:, idx2]
    s1 = xkidxg.T @ xqidx2g
    xridx3g = xru[:, idx3]
    s2 = xkidxg.T @ xridx3g
    hid = np.abs(s1[:, idx4] - s2[:, idx5])
    vsidx6g = vsu[:, idx6]
    hidq = mxq(hid, 0, "e4m3")
    y = vsidx6g.T @ hidq
    return y

@@ -1,0 +1,156 @@
+from contextlib import ExitStack
+
+import concourse.mybir as mybir
+
+F32 = mybir.dt.float32
+BF16 = mybir.dt.bfloat16
+I32 = mybir.dt.int32
+U32 = mybir.dt.uint32
+U16 = mybir.dt.uint16
+U8 = mybir.dt.uint8
+E4M3X4 = mybir.dt.float8_e4m3fn_x4
+E5M2X4 = mybir.dt.float8_e5m2_x4
+E2M1X4 = mybir.dt.float4_e2m1fn_x4
+ACT = mybir.ActivationFunctionType
+ALU = mybir.AluOpType
+
+P = 128
+PACK = 4
+K, T, I, J, N, O = 512, 1024, 512, 256, 256, 128
+QUADRANTS = 4
+
+FLOPS = 2 * K * I * J * 2 + 2 * I * N * O
+
+
+def load_scale_rows(queue, plane, scales):
+    rows = scales[0].bitcast(I32)
+    words = plane[:].bitcast(I32)
+    for q in range(QUADRANTS):
+        queue.dma_start(out=words[32 * q : 32 * q + 4, :], in_=rows[4 * q : 4 * q + 4, :])
+
+
+def tile_list_contest_rivals_looked_plain_kernel(
+    tc, xk_words, xk_scales, xq_words, xq_scales, xr_words, xr_scales, vs_words, vs_scales,
+    offs, offs2, offs3, offs4, offs5, offs6, out,
+):
+    nc = tc.nc
+    with ExitStack() as ctx:
+        keep = ctx.enter_context(tc.tile_pool(name="keep", bufs=1))
+        psum = ctx.enter_context(tc.psum_pool(name="psum", bufs=1))
+
+        key_list = keep.tile([P, I // 16], U16, name="key_list")
+        query_list = keep.tile([P, J // 16], U16, name="query_list")
+        rival_list = keep.tile([P, J // 16], U16, name="rival_list")
+        s1_list = keep.tile([P, O // 16], U16, name="s1_list")
+        s2_list = keep.tile([P, O // 16], U16, name="s2_list")
+        store_list = keep.tile([P, N // 16], U16, name="store_list")
+
+        xk_w = keep.tile([P, T], U32, name="xk_w", align_bytes=64)
+        xr_w = keep.tile([P, T], U32, name="xr_w", align_bytes=64)
+        xq_w = keep.tile([P, T], U16, name="xq_w", align_bytes=64)
+        vs_w = keep.tile([P, T], U16, name="vs_w", align_bytes=64)
+        xk_s = keep.tile([P, T], U8, name="xk_s", align_bytes=64)
+        xq_s = keep.tile([P, T], U8, name="xq_s", align_bytes=64)
+        xr_s = keep.tile([P, T], U8, name="xr_s", align_bytes=64)
+        vs_s = keep.tile([P, T], U8, name="vs_s", align_bytes=64)
+
+        nc.vector.memset(xk_s[:].bitcast(I32), 0)
+        nc.vector.memset(xq_s[:].bitcast(I32), 0)
+        nc.vector.memset(xr_s[:].bitcast(I32), 0)
+        nc.gpsimd.memset(vs_s[:].bitcast(I32), 0)
+
+        nc.sync.dma_start(query_list[:], offs2)
+        nc.sync.dma_start(out=xq_w[:].bitcast(I32), in_=xq_words[0].bitcast(I32))
+        nc.sync.dma_start(key_list[:], offs)
+        load_scale_rows(nc.sync, xk_s, xk_scales)
+        nc.sync.dma_start(out=xk_w[:].bitcast(I32), in_=xk_words[0].rearrange("p c r -> p (c r)").bitcast(I32))
+        load_scale_rows(nc.sync, xq_s, xq_scales)
+        nc.sync.dma_start(rival_list[:], offs3)
+        nc.sync.dma_start(out=xr_w[:].bitcast(I32), in_=xr_words[0].rearrange("p c r -> p (c r)").bitcast(I32))
+        load_scale_rows(nc.sync, xr_s, xr_scales)
+        nc.sync.dma_start(store_list[:], offs6)
+        nc.sync.dma_start(out=vs_w[:].bitcast(I32), in_=vs_words[0].bitcast(I32))
+        nc.sync.dma_start(s1_list[:], offs4)
+        nc.sync.dma_start(s2_list[:], offs5)
+        load_scale_rows(nc.gpsimd, vs_s, vs_scales)
+
+        xq_gw = keep.tile([P, J], U16, name="xq_gw", align_bytes=64)
+        xq_gs = keep.tile([P, J], U8, name="xq_gs", align_bytes=64)
+        xk_gw = keep.tile([P, PACK, P], U32, name="xk_gw", align_bytes=64)
+        xk_gs = keep.tile([P, PACK, P], U8, name="xk_gs", align_bytes=64)
+        xr_gw = keep.tile([P, J], U32, name="xr_gw", align_bytes=64)
+        xr_gs = keep.tile([P, J], U8, name="xr_gs", align_bytes=64)
+        vs_gw = keep.tile([P, N], U16, name="vs_gw", align_bytes=64)
+        vs_gs = keep.tile([P, N], U8, name="vs_gs", align_bytes=64)
+
+        nc.vector.tensor_copy(xq_gw[:], xq_w[:].indirect(query_list[:]))
+        nc.vector.tensor_copy(xk_gs[:].rearrange("p t m -> p m t"), xk_s[:].indirect(key_list[:]))
+        nc.vector.tensor_copy(xk_gw[:].rearrange("p t m -> p m t"), xk_w[:].indirect(key_list[:]))
+        nc.vector.tensor_copy(xq_gs[:], xq_s[:].indirect(query_list[:]))
+
+        s1_sb = [keep.tile([P, J], F32, name=f"s1_sb{t}") for t in range(PACK)]
+        s2_sb = [keep.tile([P, J], F32, name=f"s2_sb{t}") for t in range(PACK)]
+        first = keep.tile([P, PACK, O], F32, name="first", align_bytes=64)
+        diff = keep.tile([P, PACK, O], F32, name="diff", align_bytes=64)
+
+        for t in range(PACK):
+            bank = psum.tile([P, J], F32, name=f"s1_ps{t}", tag=f"bank{t}")
+            nc.tensor.matmul_mx(
+                out=bank[:],
+                lhsT=xk_gw[:, t, :].bitcast(E4M3X4), lhsT_scale=xk_gs[:, t, :],
+                rhs=xq_gw[:].bitcast(E2M1X4), rhs_scale=xq_gs[:],
+                start=True, stop=True,
+            )
+            nc.scalar.copy(s1_sb[t][:], bank[:])
+
+        nc.vector.tensor_copy(xr_gw[:], xr_w[:].indirect(rival_list[:]))
+        nc.vector.tensor_copy(xr_gs[:], xr_s[:].indirect(rival_list[:]))
+
+        s2_ps = []
+        for t in range(PACK):
+            bank = psum.tile([P, J], F32, name=f"s2_ps{t}", tag=f"bank{PACK + t}")
+            nc.tensor.matmul_mx(
+                out=bank[:],
+                lhsT=xk_gw[:, t, :].bitcast(E4M3X4), lhsT_scale=xk_gs[:, t, :],
+                rhs=xr_gw[:].bitcast(E5M2X4), rhs_scale=xr_gs[:],
+                start=True, stop=True,
+            )
+            s2_ps.append(bank)
+
+        nc.vector.tensor_copy(vs_gw[:], vs_w[:].indirect(store_list[:]))
+
+        for t in range(PACK):
+            if t < 2:
+                nc.scalar.copy(s2_sb[t][:], s2_ps[t][:])
+            else:
+                nc.vector.tensor_copy(s2_sb[t][:], s2_ps[t][:])
+            nc.scalar.activation(first[:, t, :], s1_sb[t][:].indirect(s1_list[:]), ACT.Copy)
+
+        for t in range(PACK):
+            nc.vector.tensor_tensor(diff[:, t, :], s2_sb[t][:].indirect(s2_list[:]), first[:, t, :], ALU.subtract)
+
+        hid = keep.tile([P, O, PACK], BF16, name="hid", align_bytes=64)
+        nc.scalar.activation(hid[:], diff[:].rearrange("p t o -> p o t"), ACT.Abs)
+
+        nc.vector.tensor_copy(vs_gs[:], vs_s[:].indirect(store_list[:]))
+
+        hid_w = keep.tile([P, O], U32, name="hid_w", align_bytes=64)
+        hid_s = keep.tile([P, O], U8, name="hid_s", align_bytes=64)
+        nc.vector.quantize_mx(out=hid_w[:].bitcast(E4M3X4), scales=hid_s[:], in_=hid[:].rearrange("p o t -> p (o t)"))
+
+        for h in range(N // P):
+            bank = psum.tile([P, J], F32, name=f"y_ps{h}", tag=f"bank{h}")
+            cols = slice(h * P, (h + 1) * P)
+            nc.tensor.matmul_mx(
+                out=bank[:, 0:O],
+                lhsT=vs_gw[:, cols].bitcast(E2M1X4), lhsT_scale=vs_gs[:, cols],
+                rhs=hid_w[:].bitcast(E4M3X4), rhs_scale=hid_s[:],
+                start=True, stop=True,
+            )
+            y = keep.tile([P, O], F32, name=f"y{h}")
+            if h == 0:
+                nc.vector.tensor_copy(y[:], bank[:, 0:O])
+                nc.sync.dma_start(out=out[cols, :], in_=y[:])
+            else:
+                nc.scalar.copy(y[:], bank[:, 0:O])
+                nc.scalar.dma_start(out=out[cols, :], in_=y[:])

@@ -22,11 +22,11 @@ QUADRANTS = 4
 FLOPS = 2 * K * I * J * 2 + 2 * I * N * O
 
 
-def load_scale_rows(queue, plane, scales):
+def load_scale_rows(queues, plane, scales):
     rows = scales[0].bitcast(I32)
     words = plane[:].bitcast(I32)
     for q in range(QUADRANTS):
-        queue.dma_start(out=words[32 * q : 32 * q + 4, :], in_=rows[4 * q : 4 * q + 4, :])
+        queues[q].dma_start(out=words[32 * q : 32 * q + 4, :], in_=rows[4 * q : 4 * q + 4, :])
 
 
 def tile_list_contest_rivals_looked_plain_kernel(
@@ -36,6 +36,7 @@ def tile_list_contest_rivals_looked_plain_kernel(
     nc = tc.nc
     with ExitStack() as ctx:
         keep = ctx.enter_context(tc.tile_pool(name="keep", bufs=1))
+        shared = ctx.enter_context(tc.tile_pool(name="shared", bufs=1))
         psum = ctx.enter_context(tc.psum_pool(name="psum", bufs=1))
 
         key_list = keep.tile([P, I // 16], U16, name="key_list")
@@ -48,31 +49,31 @@ def tile_list_contest_rivals_looked_plain_kernel(
         xk_w = keep.tile([P, T], U32, name="xk_w", align_bytes=64)
         xr_w = keep.tile([P, T], U32, name="xr_w", align_bytes=64)
         xq_w = keep.tile([P, T], U16, name="xq_w", align_bytes=64)
-        vs_w = keep.tile([P, T], U16, name="vs_w", align_bytes=64)
+        vs_w = shared.tile([P, T], U16, name="vs_w", offset=0, align_bytes=64)
         xk_s = keep.tile([P, T], U8, name="xk_s", align_bytes=64)
         xq_s = keep.tile([P, T], U8, name="xq_s", align_bytes=64)
         xr_s = keep.tile([P, T], U8, name="xr_s", align_bytes=64)
-        vs_s = keep.tile([P, T], U8, name="vs_s", align_bytes=64)
+        vs_s = keep.tile([P, T], U8, name="vs_s", tag="vs_s", align_bytes=64)
 
         nc.vector.memset(xk_s[:].bitcast(I32), 0)
         nc.vector.memset(xq_s[:].bitcast(I32), 0)
         nc.vector.memset(xr_s[:].bitcast(I32), 0)
-        nc.gpsimd.memset(vs_s[:].bitcast(I32), 0)
+        nc.vector.memset(vs_s[:].bitcast(I32), 0)
 
         nc.sync.dma_start(query_list[:], offs2)
-        nc.sync.dma_start(out=xq_w[:].bitcast(I32), in_=xq_words[0].bitcast(I32))
+        nc.scalar.dma_start(out=xq_w[:].bitcast(I32), in_=xq_words[0].bitcast(I32))
         nc.sync.dma_start(key_list[:], offs)
-        load_scale_rows(nc.sync, xk_s, xk_scales)
+        load_scale_rows([nc.sync, nc.sync, nc.scalar, nc.scalar], xk_s, xk_scales)
         nc.sync.dma_start(out=xk_w[:].bitcast(I32), in_=xk_words[0].rearrange("p c r -> p (c r)").bitcast(I32))
-        load_scale_rows(nc.sync, xq_s, xq_scales)
+        load_scale_rows([nc.sync] * 4, xq_s, xq_scales)
         nc.sync.dma_start(rival_list[:], offs3)
         nc.sync.dma_start(out=xr_w[:].bitcast(I32), in_=xr_words[0].rearrange("p c r -> p (c r)").bitcast(I32))
-        load_scale_rows(nc.sync, xr_s, xr_scales)
-        nc.sync.dma_start(store_list[:], offs6)
+        load_scale_rows([nc.sync] * 4, xr_s, xr_scales)
         nc.sync.dma_start(out=vs_w[:].bitcast(I32), in_=vs_words[0].bitcast(I32))
+        nc.sync.dma_start(store_list[:], offs6)
         nc.sync.dma_start(s1_list[:], offs4)
         nc.sync.dma_start(s2_list[:], offs5)
-        load_scale_rows(nc.gpsimd, vs_s, vs_scales)
+        load_scale_rows([nc.sync] * 4, vs_s, vs_scales)
 
         xq_gw = keep.tile([P, J], U16, name="xq_gw", align_bytes=64)
         xq_gs = keep.tile([P, J], U8, name="xq_gs", align_bytes=64)
@@ -81,16 +82,13 @@ def tile_list_contest_rivals_looked_plain_kernel(
         xr_gw = keep.tile([P, J], U32, name="xr_gw", align_bytes=64)
         xr_gs = keep.tile([P, J], U8, name="xr_gs", align_bytes=64)
         vs_gw = keep.tile([P, N], U16, name="vs_gw", align_bytes=64)
-        vs_gs = keep.tile([P, N], U8, name="vs_gs", align_bytes=64)
 
         nc.vector.tensor_copy(xq_gw[:], xq_w[:].indirect(query_list[:]))
         nc.vector.tensor_copy(xk_gs[:].rearrange("p t m -> p m t"), xk_s[:].indirect(key_list[:]))
         nc.vector.tensor_copy(xk_gw[:].rearrange("p t m -> p m t"), xk_w[:].indirect(key_list[:]))
         nc.vector.tensor_copy(xq_gs[:], xq_s[:].indirect(query_list[:]))
 
-        s1_sb = [keep.tile([P, J], F32, name=f"s1_sb{t}") for t in range(PACK)]
-        s2_sb = [keep.tile([P, J], F32, name=f"s2_sb{t}") for t in range(PACK)]
-        first = keep.tile([P, PACK, O], F32, name="first", align_bytes=64)
+        s1_sb = [keep.tile([P, J], F32, name=f"s1_sb{t}", tag=f"s1_sb{t}", align_bytes=64) for t in range(PACK)]
         diff = keep.tile([P, PACK, O], F32, name="diff", align_bytes=64)
 
         for t in range(PACK):
@@ -119,22 +117,26 @@ def tile_list_contest_rivals_looked_plain_kernel(
 
         nc.vector.tensor_copy(vs_gw[:], vs_w[:].indirect(store_list[:]))
 
-        for t in range(PACK):
-            if t < 2:
-                nc.scalar.copy(s2_sb[t][:], s2_ps[t][:])
-            else:
-                nc.vector.tensor_copy(s2_sb[t][:], s2_ps[t][:])
-            nc.scalar.activation(first[:, t, :], s1_sb[t][:].indirect(s1_list[:]), ACT.Copy)
-
-        for t in range(PACK):
-            nc.vector.tensor_tensor(diff[:, t, :], s2_sb[t][:].indirect(s2_list[:]), first[:, t, :], ALU.subtract)
-
         hid = keep.tile([P, O, PACK], BF16, name="hid", align_bytes=64)
-        nc.scalar.activation(hid[:], diff[:].rearrange("p t o -> p o t"), ACT.Abs)
+        for t in range(PACK):
+            first = keep.tile([P, O], F32, name=f"first{t}", align_bytes=64)
+            if t < 2:
+                s2_sb = shared.tile([P, J], F32, name=f"s2_sb{t}", offset=4 * J * t, align_bytes=64)
+                nc.scalar.activation(first[:], s1_sb[t][:].indirect(s1_list[:]), ACT.Copy)
+                nc.vector.tensor_copy(s2_sb[:], s2_ps[t][:])
+            else:
+                s2_sb = keep.tile([P, J], F32, name=f"s2_sb{t}", tag=f"s1_sb{t - 1}", align_bytes=64)
+                nc.scalar.copy(s2_sb[:], s2_ps[t][:])
+                nc.scalar.activation(first[:], s1_sb[t][:].indirect(s1_list[:]), ACT.Copy)
+            nc.vector.tensor_tensor(diff[:, t, :], s2_sb[:].indirect(s2_list[:]), first[:], ALU.subtract)
+            if t % 2 == 1:
+                pair = slice(t - 1, t + 1)
+                nc.scalar.activation(hid[:, :, pair], diff[:, pair, :].rearrange("p t o -> p o t"), ACT.Abs)
 
+        vs_gs = keep.tile([P, N], U8, name="vs_gs", align_bytes=64)
         nc.vector.tensor_copy(vs_gs[:], vs_s[:].indirect(store_list[:]))
 
-        hid_w = keep.tile([P, O], U32, name="hid_w", align_bytes=64)
+        hid_w = keep.tile([P, O], U32, name="hid_w", tag="vs_s", align_bytes=64)
         hid_s = keep.tile([P, O], U8, name="hid_s", align_bytes=64)
         nc.vector.quantize_mx(out=hid_w[:].bitcast(E4M3X4), scales=hid_s[:], in_=hid[:].rearrange("p o t -> p (o t)"))
 

@@ -16,17 +16,24 @@ ALU = mybir.AluOpType
 
 P = 128
 PACK = 4
-K, T, I, J, N, O = 512, 1024, 512, 256, 256, 128
-QUADRANTS = 4
+QUADRANT = 32
+LIST_ROWS = 16
+MX_ALIGN = 64
+K = 512
+COLUMNS = 1024
+I = 512
+J = 256
+N = 256
+O = 128
 
-FLOPS = 2 * K * I * J * 2 + 2 * I * N * O
+FLOPS = 2 * (2 * K * I * J) + 2 * I * N * O
 
 
-def load_scale_rows(queues, plane, scales):
+def load_scale_rows(nc, tile, scales):
     rows = scales[0].bitcast(I32)
-    words = plane[:].bitcast(I32)
-    for q in range(QUADRANTS):
-        queues[q].dma_start(out=words[32 * q : 32 * q + 4, :], in_=rows[4 * q : 4 * q + 4, :])
+    dst = tile[:].bitcast(I32)
+    for q in range(P // QUADRANT):
+        nc.sync.dma_start(out=dst[QUADRANT * q : QUADRANT * q + PACK, :], in_=rows[PACK * q : PACK * (q + 1), :])
 
 
 def tile_list_contest_rivals_looked_plain_kernel(
@@ -36,123 +43,114 @@ def tile_list_contest_rivals_looked_plain_kernel(
     nc = tc.nc
     with ExitStack() as ctx:
         keep = ctx.enter_context(tc.tile_pool(name="keep", bufs=1))
-        shared = ctx.enter_context(tc.tile_pool(name="shared", bufs=1))
         psum = ctx.enter_context(tc.psum_pool(name="psum", bufs=1))
 
-        key_list = keep.tile([P, I // 16], U16, name="key_list")
-        query_list = keep.tile([P, J // 16], U16, name="query_list")
-        rival_list = keep.tile([P, J // 16], U16, name="rival_list")
-        s1_list = keep.tile([P, O // 16], U16, name="s1_list")
-        s2_list = keep.tile([P, O // 16], U16, name="s2_list")
-        store_list = keep.tile([P, N // 16], U16, name="store_list")
+        key_list = keep.tile([P, I // LIST_ROWS], U16, name="key_list")
+        query_list = keep.tile([P, J // LIST_ROWS], U16, name="query_list")
+        rival_list = keep.tile([P, J // LIST_ROWS], U16, name="rival_list")
+        s1_list = keep.tile([P, O // LIST_ROWS], U16, name="s1_list")
+        s2_list = keep.tile([P, O // LIST_ROWS], U16, name="s2_list")
+        store_list = keep.tile([P, N // LIST_ROWS], U16, name="store_list")
 
-        xk_w = keep.tile([P, T], U32, name="xk_w", align_bytes=64)
-        xr_w = keep.tile([P, T], U32, name="xr_w", align_bytes=64)
-        xq_w = keep.tile([P, T], U16, name="xq_w", align_bytes=64)
-        vs_w = shared.tile([P, T], U16, name="vs_w", offset=0, align_bytes=64)
-        xk_s = keep.tile([P, T], U8, name="xk_s", align_bytes=64)
-        xq_s = keep.tile([P, T], U8, name="xq_s", align_bytes=64)
-        xr_s = keep.tile([P, T], U8, name="xr_s", align_bytes=64)
-        vs_s = keep.tile([P, T], U8, name="vs_s", tag="vs_s", align_bytes=64)
+        xk_w = keep.tile([P, COLUMNS], U32, name="xk_w", align_bytes=MX_ALIGN)
+        xr_w = keep.tile([P, COLUMNS], U32, name="xr_w", align_bytes=MX_ALIGN)
+        xq_w = keep.tile([P, COLUMNS], U16, name="xq_w", align_bytes=MX_ALIGN)
+        vs_w = keep.tile([P, COLUMNS], U16, name="vs_w", align_bytes=MX_ALIGN)
+        xk_s = keep.tile([P, COLUMNS], U8, name="xk_s", align_bytes=MX_ALIGN)
+        xq_s = keep.tile([P, COLUMNS], U8, name="xq_s", align_bytes=MX_ALIGN)
+        xr_s = keep.tile([P, COLUMNS], U8, name="xr_s", align_bytes=MX_ALIGN)
+        vs_s = keep.tile([P, COLUMNS], U8, name="vs_s", tag="vs_s_then_hid_w", align_bytes=MX_ALIGN)
 
-        nc.vector.memset(xk_s[:].bitcast(I32), 0)
-        nc.vector.memset(xq_s[:].bitcast(I32), 0)
-        nc.vector.memset(xr_s[:].bitcast(I32), 0)
-        nc.vector.memset(vs_s[:].bitcast(I32), 0)
+        for tile in (xk_s, xq_s, xr_s, vs_s):
+            nc.vector.memset(tile[:].bitcast(I32), 0)
 
         nc.sync.dma_start(query_list[:], offs2)
         nc.scalar.dma_start(out=xq_w[:].bitcast(I32), in_=xq_words[0].bitcast(I32))
         nc.sync.dma_start(key_list[:], offs)
-        load_scale_rows([nc.sync, nc.sync, nc.scalar, nc.scalar], xk_s, xk_scales)
+        load_scale_rows(nc, xk_s, xk_scales)
         nc.sync.dma_start(out=xk_w[:].bitcast(I32), in_=xk_words[0].rearrange("p c r -> p (c r)").bitcast(I32))
-        load_scale_rows([nc.sync] * 4, xq_s, xq_scales)
+        load_scale_rows(nc, xq_s, xq_scales)
         nc.sync.dma_start(rival_list[:], offs3)
         nc.sync.dma_start(out=xr_w[:].bitcast(I32), in_=xr_words[0].rearrange("p c r -> p (c r)").bitcast(I32))
-        load_scale_rows([nc.sync] * 4, xr_s, xr_scales)
+        load_scale_rows(nc, xr_s, xr_scales)
         nc.sync.dma_start(out=vs_w[:].bitcast(I32), in_=vs_words[0].bitcast(I32))
         nc.sync.dma_start(store_list[:], offs6)
         nc.sync.dma_start(s1_list[:], offs4)
         nc.sync.dma_start(s2_list[:], offs5)
-        load_scale_rows([nc.sync] * 4, vs_s, vs_scales)
+        load_scale_rows(nc, vs_s, vs_scales)
 
-        xq_gw = keep.tile([P, J], U16, name="xq_gw", align_bytes=64)
-        xq_gs = keep.tile([P, J], U8, name="xq_gs", align_bytes=64)
-        xk_gw = keep.tile([P, PACK, P], U32, name="xk_gw", align_bytes=64)
-        xk_gs = keep.tile([P, PACK, P], U8, name="xk_gs", align_bytes=64)
-        xr_gw = keep.tile([P, J], U32, name="xr_gw", align_bytes=64)
-        xr_gs = keep.tile([P, J], U8, name="xr_gs", align_bytes=64)
-        vs_gw = keep.tile([P, N], U16, name="vs_gw", align_bytes=64)
+        xq_gw = keep.tile([P, J], U16, name="xq_gw", align_bytes=MX_ALIGN)
+        xq_gs = keep.tile([P, J], U8, name="xq_gs", align_bytes=MX_ALIGN)
+        xk_gw = keep.tile([P, PACK, P], U32, name="xk_gw", align_bytes=MX_ALIGN)
+        xk_gs = keep.tile([P, PACK, P], U8, name="xk_gs", align_bytes=MX_ALIGN)
+        xr_gw = keep.tile([P, J], U32, name="xr_gw", align_bytes=MX_ALIGN)
+        xr_gs = keep.tile([P, J], U8, name="xr_gs", align_bytes=MX_ALIGN)
+        vs_gw = keep.tile([P, N], U16, name="vs_gw", align_bytes=MX_ALIGN)
+        vs_gs = keep.tile([P, N], U8, name="vs_gs", align_bytes=MX_ALIGN)
 
         nc.vector.tensor_copy(xq_gw[:], xq_w[:].indirect(query_list[:]))
         nc.vector.tensor_copy(xk_gs[:].rearrange("p t m -> p m t"), xk_s[:].indirect(key_list[:]))
         nc.vector.tensor_copy(xk_gw[:].rearrange("p t m -> p m t"), xk_w[:].indirect(key_list[:]))
         nc.vector.tensor_copy(xq_gs[:], xq_s[:].indirect(query_list[:]))
 
-        s1_sb = [keep.tile([P, J], F32, name=f"s1_sb{t}", tag=f"s1_sb{t}", align_bytes=64) for t in range(PACK)]
-        diff = keep.tile([P, PACK, O], F32, name="diff", align_bytes=64)
+        def scores(name, words, scales, first_bank):
+            tiles = []
+            for t in range(PACK):
+                bank = psum.tile([P, J], F32, name=f"{name}_ps{t}", tag=f"bank{first_bank + t}")
+                nc.tensor.matmul_mx(
+                    out=bank[:],
+                    lhsT=xk_gw[:, t, :].bitcast(E4M3X4), lhsT_scale=xk_gs[:, t, :],
+                    rhs=words, rhs_scale=scales,
+                    start=True, stop=True,
+                )
+                tile = keep.tile([P, J], F32, name=f"{name}_sb{t}", align_bytes=MX_ALIGN)
+                nc.scalar.copy(tile[:], bank[:])
+                tiles.append(tile)
+            return tiles
 
-        for t in range(PACK):
-            bank = psum.tile([P, J], F32, name=f"s1_ps{t}", tag=f"bank{t}")
-            nc.tensor.matmul_mx(
-                out=bank[:],
-                lhsT=xk_gw[:, t, :].bitcast(E4M3X4), lhsT_scale=xk_gs[:, t, :],
-                rhs=xq_gw[:].bitcast(E2M1X4), rhs_scale=xq_gs[:],
-                start=True, stop=True,
-            )
-            nc.scalar.copy(s1_sb[t][:], bank[:])
+        s1 = scores("s1", xq_gw[:].bitcast(E2M1X4), xq_gs[:], first_bank=0)
 
         nc.vector.tensor_copy(xr_gw[:], xr_w[:].indirect(rival_list[:]))
         nc.vector.tensor_copy(xr_gs[:], xr_s[:].indirect(rival_list[:]))
-
-        s2_ps = []
-        for t in range(PACK):
-            bank = psum.tile([P, J], F32, name=f"s2_ps{t}", tag=f"bank{PACK + t}")
-            nc.tensor.matmul_mx(
-                out=bank[:],
-                lhsT=xk_gw[:, t, :].bitcast(E4M3X4), lhsT_scale=xk_gs[:, t, :],
-                rhs=xr_gw[:].bitcast(E5M2X4), rhs_scale=xr_gs[:],
-                start=True, stop=True,
-            )
-            s2_ps.append(bank)
+        s2 = scores("s2", xr_gw[:].bitcast(E5M2X4), xr_gs[:], first_bank=PACK)
 
         nc.vector.tensor_copy(vs_gw[:], vs_w[:].indirect(store_list[:]))
 
-        hid = keep.tile([P, O, PACK], BF16, name="hid", align_bytes=64)
+        s1_picked = []
         for t in range(PACK):
-            first = keep.tile([P, O], F32, name=f"first{t}", align_bytes=64)
-            if t < 2:
-                s2_sb = shared.tile([P, J], F32, name=f"s2_sb{t}", offset=4 * J * t, align_bytes=64)
-                nc.scalar.activation(first[:], s1_sb[t][:].indirect(s1_list[:]), ACT.Copy)
-                nc.vector.tensor_copy(s2_sb[:], s2_ps[t][:])
+            picked = keep.tile([P, O], F32, name=f"s1_picked{t}", align_bytes=MX_ALIGN)
+            if t < PACK - 1:
+                nc.vector.tensor_copy(picked[:], s1[t][:].indirect(s1_list[:]))
             else:
-                s2_sb = keep.tile([P, J], F32, name=f"s2_sb{t}", tag=f"s1_sb{t - 1}", align_bytes=64)
-                nc.scalar.copy(s2_sb[:], s2_ps[t][:])
-                nc.scalar.activation(first[:], s1_sb[t][:].indirect(s1_list[:]), ACT.Copy)
-            nc.vector.tensor_tensor(diff[:, t, :], s2_sb[:].indirect(s2_list[:]), first[:], ALU.subtract)
+                nc.scalar.activation(picked[:], s1[t][:].indirect(s1_list[:]), ACT.Copy)
+            s1_picked.append(picked)
+
+        diff = keep.tile([P, PACK, O], F32, name="diff", align_bytes=MX_ALIGN)
+        hid = keep.tile([P, O, PACK], BF16, name="hid", align_bytes=MX_ALIGN)
+        for t in range(PACK):
+            nc.vector.tensor_tensor(diff[:, t, :], s2[t][:].indirect(s2_list[:]), s1_picked[t][:], ALU.subtract)
             if t % 2 == 1:
                 pair = slice(t - 1, t + 1)
                 nc.scalar.activation(hid[:, :, pair], diff[:, pair, :].rearrange("p t o -> p o t"), ACT.Abs)
 
-        vs_gs = keep.tile([P, N], U8, name="vs_gs", align_bytes=64)
         nc.vector.tensor_copy(vs_gs[:], vs_s[:].indirect(store_list[:]))
-
-        hid_w = keep.tile([P, O], U32, name="hid_w", tag="vs_s", align_bytes=64)
-        hid_s = keep.tile([P, O], U8, name="hid_s", align_bytes=64)
+        hid_w = keep.tile([P, O], U32, name="hid_w", tag="vs_s_then_hid_w", align_bytes=MX_ALIGN)
+        hid_s = keep.tile([P, O], U8, name="hid_s", align_bytes=MX_ALIGN)
         nc.vector.quantize_mx(out=hid_w[:].bitcast(E4M3X4), scales=hid_s[:], in_=hid[:].rearrange("p o t -> p (o t)"))
 
-        for h in range(N // P):
-            bank = psum.tile([P, J], F32, name=f"y_ps{h}", tag=f"bank{h}")
-            cols = slice(h * P, (h + 1) * P)
+        for half in range(N // P):
+            rows = slice(half * P, (half + 1) * P)
+            bank = psum.tile([P, J], F32, name=f"out_ps{half}", tag=f"bank{half}")
             nc.tensor.matmul_mx(
                 out=bank[:, 0:O],
-                lhsT=vs_gw[:, cols].bitcast(E2M1X4), lhsT_scale=vs_gs[:, cols],
+                lhsT=vs_gw[:, rows].bitcast(E2M1X4), lhsT_scale=vs_gs[:, rows],
                 rhs=hid_w[:].bitcast(E4M3X4), rhs_scale=hid_s[:],
                 start=True, stop=True,
             )
-            y = keep.tile([P, O], F32, name=f"y{h}")
-            if h == 0:
-                nc.vector.tensor_copy(y[:], bank[:, 0:O])
-                nc.sync.dma_start(out=out[cols, :], in_=y[:])
+            result = keep.tile([P, O], F32, name=f"result{half}")
+            if half == 0:
+                nc.vector.tensor_copy(result[:], bank[:, 0:O])
+                nc.sync.dma_start(out=out[rows, :], in_=result[:])
             else:
-                nc.scalar.copy(y[:], bank[:, 0:O])
-                nc.scalar.dma_start(out=out[cols, :], in_=y[:])
+                nc.scalar.copy(result[:], bank[:, 0:O])
+                nc.scalar.dma_start(out=out[rows, :], in_=result[:])

from contextlib import ExitStack

import concourse.mybir as mybir

F32 = mybir.dt.float32
BF16 = mybir.dt.bfloat16
I32 = mybir.dt.int32
U32 = mybir.dt.uint32
U16 = mybir.dt.uint16
U8 = mybir.dt.uint8
E4M3X4 = mybir.dt.float8_e4m3fn_x4
E5M2X4 = mybir.dt.float8_e5m2_x4
E2M1X4 = mybir.dt.float4_e2m1fn_x4
ACT = mybir.ActivationFunctionType
ALU = mybir.AluOpType

P = 128
PACK = 4
QUADRANT = 32
LIST_ROWS = 16
MX_ALIGN = 64
K = 512
COLUMNS = 1024
I = 512
J = 256
N = 256
O = 128

FLOPS = 2 * (2 * K * I * J) + 2 * I * N * O


def load_scale_rows(nc, tile, scales):
    rows = scales[0].bitcast(I32)
    dst = tile[:].bitcast(I32)
    for q in range(P // QUADRANT):
        nc.sync.dma_start(out=dst[QUADRANT * q : QUADRANT * q + PACK, :], in_=rows[PACK * q : PACK * (q + 1), :])


def tile_list_contest_rivals_looked_plain_kernel(
    tc, xk_words, xk_scales, xq_words, xq_scales, xr_words, xr_scales, vs_words, vs_scales,
    offs, offs2, offs3, offs4, offs5, offs6, out,
):
    nc = tc.nc
    with ExitStack() as ctx:
        keep = ctx.enter_context(tc.tile_pool(name="keep", bufs=1))
        psum = ctx.enter_context(tc.psum_pool(name="psum", bufs=1))

        key_list = keep.tile([P, I // LIST_ROWS], U16, name="key_list")
        query_list = keep.tile([P, J // LIST_ROWS], U16, name="query_list")
        rival_list = keep.tile([P, J // LIST_ROWS], U16, name="rival_list")
        s1_list = keep.tile([P, O // LIST_ROWS], U16, name="s1_list")
        s2_list = keep.tile([P, O // LIST_ROWS], U16, name="s2_list")
        store_list = keep.tile([P, N // LIST_ROWS], U16, name="store_list")

        xk_w = keep.tile([P, COLUMNS], U32, name="xk_w", align_bytes=MX_ALIGN)
        xr_w = keep.tile([P, COLUMNS], U32, name="xr_w", align_bytes=MX_ALIGN)
        xq_w = keep.tile([P, COLUMNS], U16, name="xq_w", align_bytes=MX_ALIGN)
        vs_w = keep.tile([P, COLUMNS], U16, name="vs_w", align_bytes=MX_ALIGN)
        xk_s = keep.tile([P, COLUMNS], U8, name="xk_s", align_bytes=MX_ALIGN)
        xq_s = keep.tile([P, COLUMNS], U8, name="xq_s", align_bytes=MX_ALIGN)
        xr_s = keep.tile([P, COLUMNS], U8, name="xr_s", align_bytes=MX_ALIGN)
        vs_s = keep.tile([P, COLUMNS], U8, name="vs_s", tag="vs_s_then_hid_w", align_bytes=MX_ALIGN)

        for tile in (xk_s, xq_s, xr_s, vs_s):
            nc.vector.memset(tile[:].bitcast(I32), 0)

        nc.sync.dma_start(query_list[:], offs2)
        nc.scalar.dma_start(out=xq_w[:].bitcast(I32), in_=xq_words[0].bitcast(I32))
        nc.sync.dma_start(key_list[:], offs)
        load_scale_rows(nc, xk_s, xk_scales)
        nc.sync.dma_start(out=xk_w[:].bitcast(I32), in_=xk_words[0].rearrange("p c r -> p (c r)").bitcast(I32))
        load_scale_rows(nc, xq_s, xq_scales)
        nc.sync.dma_start(rival_list[:], offs3)
        nc.sync.dma_start(out=xr_w[:].bitcast(I32), in_=xr_words[0].rearrange("p c r -> p (c r)").bitcast(I32))
        load_scale_rows(nc, xr_s, xr_scales)
        nc.sync.dma_start(out=vs_w[:].bitcast(I32), in_=vs_words[0].bitcast(I32))
        nc.sync.dma_start(store_list[:], offs6)
        nc.sync.dma_start(s1_list[:], offs4)
        nc.sync.dma_start(s2_list[:], offs5)
        load_scale_rows(nc, vs_s, vs_scales)

        xq_gw = keep.tile([P, J], U16, name="xq_gw", align_bytes=MX_ALIGN)
        xq_gs = keep.tile([P, J], U8, name="xq_gs", align_bytes=MX_ALIGN)
        xk_gw = keep.tile([P, PACK, P], U32, name="xk_gw", align_bytes=MX_ALIGN)
        xk_gs = keep.tile([P, PACK, P], U8, name="xk_gs", align_bytes=MX_ALIGN)
        xr_gw = keep.tile([P, J], U32, name="xr_gw", align_bytes=MX_ALIGN)
        xr_gs = keep.tile([P, J], U8, name="xr_gs", align_bytes=MX_ALIGN)
        vs_gw = keep.tile([P, N], U16, name="vs_gw", align_bytes=MX_ALIGN)
        vs_gs = keep.tile([P, N], U8, name="vs_gs", align_bytes=MX_ALIGN)

        nc.vector.tensor_copy(xq_gw[:], xq_w[:].indirect(query_list[:]))
        nc.vector.tensor_copy(xk_gs[:].rearrange("p t m -> p m t"), xk_s[:].indirect(key_list[:]))
        nc.vector.tensor_copy(xk_gw[:].rearrange("p t m -> p m t"), xk_w[:].indirect(key_list[:]))
        nc.vector.tensor_copy(xq_gs[:], xq_s[:].indirect(query_list[:]))

        def scores(name, words, scales, first_bank):
            tiles = []
            for t in range(PACK):
                bank = psum.tile([P, J], F32, name=f"{name}_ps{t}", tag=f"bank{first_bank + t}")
                nc.tensor.matmul_mx(
                    out=bank[:],
                    lhsT=xk_gw[:, t, :].bitcast(E4M3X4), lhsT_scale=xk_gs[:, t, :],
                    rhs=words, rhs_scale=scales,
                    start=True, stop=True,
                )
                tile = keep.tile([P, J], F32, name=f"{name}_sb{t}", align_bytes=MX_ALIGN)
                nc.scalar.copy(tile[:], bank[:])
                tiles.append(tile)
            return tiles

        s1 = scores("s1", xq_gw[:].bitcast(E2M1X4), xq_gs[:], first_bank=0)

        nc.vector.tensor_copy(xr_gw[:], xr_w[:].indirect(rival_list[:]))
        nc.vector.tensor_copy(xr_gs[:], xr_s[:].indirect(rival_list[:]))
        s2 = scores("s2", xr_gw[:].bitcast(E5M2X4), xr_gs[:], first_bank=PACK)

        nc.vector.tensor_copy(vs_gw[:], vs_w[:].indirect(store_list[:]))

        s1_picked = []
        for t in range(PACK):
            picked = keep.tile([P, O], F32, name=f"s1_picked{t}", align_bytes=MX_ALIGN)
            if t < PACK - 1:
                nc.vector.tensor_copy(picked[:], s1[t][:].indirect(s1_list[:]))
            else:
                nc.scalar.activation(picked[:], s1[t][:].indirect(s1_list[:]), ACT.Copy)
            s1_picked.append(picked)

        diff = keep.tile([P, PACK, O], F32, name="diff", align_bytes=MX_ALIGN)
        hid = keep.tile([P, O, PACK], BF16, name="hid", align_bytes=MX_ALIGN)
        for t in range(PACK):
            nc.vector.tensor_tensor(diff[:, t, :], s2[t][:].indirect(s2_list[:]), s1_picked[t][:], ALU.subtract)
            if t % 2 == 1:
                pair = slice(t - 1, t + 1)
                nc.scalar.activation(hid[:, :, pair], diff[:, pair, :].rearrange("p t o -> p o t"), ACT.Abs)

        nc.vector.tensor_copy(vs_gs[:], vs_s[:].indirect(store_list[:]))
        hid_w = keep.tile([P, O], U32, name="hid_w", tag="vs_s_then_hid_w", align_bytes=MX_ALIGN)
        hid_s = keep.tile([P, O], U8, name="hid_s", align_bytes=MX_ALIGN)
        nc.vector.quantize_mx(out=hid_w[:].bitcast(E4M3X4), scales=hid_s[:], in_=hid[:].rearrange("p o t -> p (o t)"))

        for half in range(N // P):
            rows = slice(half * P, (half + 1) * P)
            bank = psum.tile([P, J], F32, name=f"out_ps{half}", tag=f"bank{half}")
            nc.tensor.matmul_mx(
                out=bank[:, 0:O],
                lhsT=vs_gw[:, rows].bitcast(E2M1X4), lhsT_scale=vs_gs[:, rows],
                rhs=hid_w[:].bitcast(E4M3X4), rhs_scale=hid_s[:],
                start=True, stop=True,
            )
            result = keep.tile([P, O], F32, name=f"result{half}")
            if half == 0:
                nc.vector.tensor_copy(result[:], bank[:, 0:O])
                nc.sync.dma_start(out=out[rows, :], in_=result[:])
            else:
                nc.scalar.copy(result[:], bank[:, 0:O])
                nc.scalar.dma_start(out=out[rows, :], in_=result[:])
